import numpy as np, ml_dtypes
CORES = [24,25,26,27,28,29,30,31]
N = 8
import mx_ref
BF = ml_dtypes.bfloat16
def gcols(t, e):
    v = np.concatenate([t.reshape(8, 16, -1, 4), np.zeros((8, 16, 1, 4), BF)], axis=2)
    return np.ascontiguousarray(np.stack([v[g][:, e[g]] for g in range(8)])).reshape(128, -1)
def tile(rs):
    return np.stack(rs, axis=2).reshape(128, -1).astype(BF)
def f(rng, *shape):
    return mx_ref.flush((rng.standard_normal(shape, dtype=np.float32) * np.exp2(rng.integers(-2, 3, shape[:-1] + (1,)))).astype(BF))
def wide(rng, *shape, cols=0):
    v = rng.standard_normal(shape, dtype=np.float32) * np.exp2(rng.integers(-12, 13, shape)).astype(np.float32)
    if cols: v *= np.repeat(np.exp2(rng.integers(-cols, cols + 1, shape[:-2] + (1, shape[-1] // 4))) * (rng.random(shape[:-2] + (1, shape[-1] // 4)) > 0.0625), 4, axis=-1).astype(np.float32)
    return mx_ref.flush(v.astype(BF))
T, SH = 256, 32
def shifts(s):
    return np.stack([np.repeat(s, 16, axis=0).astype(np.int32)] * N)
def setup_inputs(rng):
    return {"x": f(rng, N, 128, 4 * T), "w": np.stack([f(rng, 128, 6144)] * N), "v": f(rng, N, 128, 512), "sf": shifts(rng.integers(0, SH + 1, (8, 3)))}
def setup_inputs_zero(rng):
    d = setup_inputs(rng); s = np.zeros((8, 3), int); s[rng.integers(0, 8, 3), np.arange(3)] = SH
    d["sf"] = shifts(s); return d
def setup_inputs_most(rng):
    d = setup_inputs(rng); d["sf"] = shifts(np.full((8, 3), SH)); return d
def setup_inputs_ramp(rng):
    d = setup_inputs(rng); d["sf"] = shifts(np.stack([np.arange(8) * SH // 7] * 3, axis=1)); return d
def setup_inputs_swap(rng):
    d = setup_inputs(rng); s = rng.permutation(8) % 2 * SH
    d["sf"] = shifts(np.stack([s, SH - s, s], axis=1)); return d
def setup_inputs_spread(rng):
    d = setup_inputs(rng); d["x"] = wide(rng, N, 128, 4 * T, cols=6); return d
def check_inputs(d):
    b = []
    s = d["sf"]; g = s.reshape(N, 8, 16, 3)
    if s.min() < 0 or s.max() > SH or (g != g[:, :, :1]).any() or (s != s[:1]).any(): b.append("sf")
    if (d["w"] != d["w"][:1]).any(): b.append("w")
    return b
def reference(x, w, v, sf):
    u = [x[r] for r in range(N)]; j = np.arange(T)
    for l in range(3):
        made = []
        for r in range(N):
            s = sf[r][::16, l:l + 1]
            P = gcols(u[r], np.where(j >= s, j - s, -1))
            F = gcols(u[r - 1], np.where(j < s, T + j - s, -1)) if r > 0 else np.zeros((128, 4 * T), BF)
            qp, qf = mx_ref.quantize(P), mx_ref.quantize(F)
            R = []
            for i in range(4):
                W = mx_ref.quantize(np.ascontiguousarray(w[r][:, 2048 * l + 512 * i:2048 * l + 512 * i + 512]))
                Z = np.maximum(mx_ref.matmul(W, qp), np.float32(0)) + np.maximum(mx_ref.matmul(W, qf), np.float32(0))
                R.append(Z * np.float32(0.05))
            made.append(tile(R))
        u = made
    return {"y": np.stack([mx_ref.matmul(mx_ref.quantize(v[r]), mx_ref.quantize(u[r])) for r in range(N)])}

from concourse.mybir import dt, AluOpType, ActivationFunctionType

SCRATCH = {
    "xu": ("sbuf", [128, 1280], "bfloat16"),
    "g0": ("sbuf", [128, 1152], "bfloat16"),
    "q0": ("sbuf", [128, 384], "float8_e4m3fn_x4"),
    "s0": ("sbuf", [128, 384], "uint8"),
    "u1": ("sbuf", [128, 1408], "bfloat16"),
    "g1": ("sbuf", [128, 1280], "bfloat16"),
    "q1": ("sbuf", [128, 320], "float8_e4m3fn_x4"),
    "s1": ("sbuf", [128, 320], "uint8"),
    "u2": ("sbuf", [128, 1280], "bfloat16"),
    "g2": ("sbuf", [128, 1152], "bfloat16"),
    "q2": ("sbuf", [128, 288], "float8_e4m3fn_x4"),
    "s2": ("sbuf", [128, 288], "uint8"),
    "u3": ("sbuf", [128, 1024], "bfloat16"),
    "q3": ("sbuf", [128, 256], "float8_e4m3fn_x4"),
    "s3": ("sbuf", [128, 256], "uint8"),
    "wb": ("sbuf", [128, 6144], "bfloat16"),
    "qw": ("sbuf", [128, 1536], "float8_e4m3fn_x4"),
    "sw": ("sbuf", [128, 1536], "uint8"),
    "vb": ("sbuf", [128, 512], "bfloat16"),
    "qv": ("sbuf", [128, 128], "float8_e4m3fn_x4"),
    "sv": ("sbuf", [128, 128], "uint8"),
    "sft": ("sbuf", [128, 3], "int32"),
    "step": ("sbuf", [128, 64], "int32"),
    "part": ("sbuf", [128, 1], "int32"),
    "low": ("sbuf", [128, 1], "int32"),
    "lowf": ("sbuf", [128, 1], "float32"),
    "base": ("sbuf", [128, 3], "float32"),
    "off": ("sbuf", [128, 192], "uint16"),
    "fp": ("sbuf", [128, 768], "float32"),
    "fs": ("sbuf", [128, 384], "float32"),
    "yt": ("sbuf", [128, 256], "float32"),
    "pm": ("psum", [128, 2048], "float32"),
    "pc": ("psum", [128, 2048], "float32"),
}
LOADS = ["sf", "xh", "xl", "w0a", "w0b", "w1a", "w1b", "w2a", "w2b", "v"]
SEMAPHORES = ["qv", "qs", "qt", "qg", "rcv", "snt", "yh", "yl"] + ["ld_" + n for n in LOADS]
SH = 32
C = 0.05
MAIN = ["vvss", "ssvs", "ssvs"]
PAIR = ["ssss", "svss", "sssv"]
HALO = ["svss", "ssvs", ""]
REST = ["", "vsss", "ssss"]
CUT = {"send": 256, "x": 80, "m1": 240, "m2": 200, "c2": 104}


def rank_program(g, core, T, topo):
    rank = T.rank_of(core)
    if rank is None:
        return
    first, last = rank == 0, rank == len(T.cores) - 1
    eng = {"v": g.vector, "s": g.scalar, "t": g.tensor, "g": g, "y": g.sync}
    done = {"v": 0, "s": 0, "t": 0, "g": 0}
    known = {q: {} for q in eng}
    past = {}

    def cover(a, b):
        return a != b and past.get(a, {}).get(b[0], 0) >= b[1]

    def need(q, deps):
        best = {}
        for s, n in deps:
            best[s] = max(n, best.get(s, 0))
        todo = [(s, n) for s, n in best.items() if known[q].get(s, 0) < n]
        todo = [d for d in todo if not any(cover(e, d) for e in todo)]
        for s, n in todo:
            eng[q].wait_ge(T.sem[s], n)
            for a, b in list(past.get((s, n), {}).items()) + [(s, n)]:
                known[q][a] = max(b, known[q].get(a, 0))

    def do(q, deps, call):
        need(q, deps)
        ins = call(eng[q])
        done[q] += 1
        s = "q" + q
        ins.then_inc(T.sem[s], 1)
        past[(s, done[q])] = dict(known[q])
        past[(s, done[q])][s] = done[q]
        return (s, done[q])

    def dma(q, sem, deps, out, in_):
        need(q, deps)
        eng[q].dma_start(out, in_).then_inc(T.sem[sem], 16)
        past[(sem, 16)] = dict(known[q])
        return (sem, 16)

    ld = {}
    ld["sf"] = dma("y", "ld_sf", [], T.sft[:], T.sf[:])
    ld["xh"] = dma("s", "ld_xh", [], T.xu[:, 640:1152], T.x[:, 512:1024])
    ld["xl"] = dma("y", "ld_xl", [], T.xu[:, 128:640], T.x[:, 0:512])
    ld["w0a"] = dma("s", "ld_w0a", [], T.wb[:, 0:1024], T.w[:, 0:1024])
    ld["w0b"] = dma("y", "ld_w0b", [], T.wb[:, 1024:2048], T.w[:, 1024:2048])

    i1 = do("g", [], lambda e: e.iota(T.part[:], [[0, 1]], 0, 1))
    i2 = do("g", [], lambda e: e.iota(T.step[:], [[16, 64]], 0, 0))
    zr = []
    for ap in [T.xu[:, 1152:1280], T.xu[:, 0:128], T.u1[:, 256:384], T.u2[:, 128:256]]:
        zr.append(do("v", [], lambda e, ap=ap: e.memset(ap, 0.0)))
    if first:
        zr.append(do("v", [], lambda e: e.memset(T.g1[:, 0:256], 0.0)))
        zr.append(do("v", [], lambda e: e.memset(T.g2[:, 0:128], 0.0)))
    t = do("v", [i1], lambda e: e.tensor_scalar(T.low[:], T.part[:], 15, None, AluOpType.bitwise_and))
    t = do("v", [t], lambda e: e.tensor_scalar(T.lowf[:], T.low[:], 128.0, None, AluOpType.add))
    bs = do("v", [t, ld["sf"]], lambda e: e.tensor_scalar(
        T.base[:], T.sft[:], -4.0, T.lowf[:, 0:1], AluOpType.mult, AluOpType.add))

    def lists(l):
        return do("v", [bs, i2], lambda e: e.tensor_scalar(
            T.off[:, 64 * l:64 * l + 64], T.step[:], T.base[:, l:l + 1], None, AluOpType.add))
    off = {0: lists(0)}

    def gather(q, l, u, gt, k0, k1, g0, deps):
        out = gt[:, 4 * (k0 - g0):4 * (k1 - g0)]
        win = u[:, 4 * (k0 - SH):4 * k1].indirect(T.off[:, 64 * l:64 * l + (k1 - k0) // 4])
        if q == "v":
            return do("v", deps + [off[l]], lambda e: e.tensor_copy(out, win))
        return do("s", deps + [off[l]], lambda e: e.activation(out, win, ActivationFunctionType.Copy))

    def quant(q, s, a, b, src, s0, deps):
        return do("v", deps, lambda e: e.quantize_mx(q[:, a:b], s[:, a:b], src[:, 4 * s0:4 * (s0 + b - a)]))

    W = {}

    def quant_w(l, i0, i1, name):
        c = 512 * l
        t = quant(T.qw, T.sw, c + 128 * i0, c + 128 * i1, T.wb, c + 128 * i0, [ld[name]])
        for i in range(i0, i1):
            W[l, i] = t

    def mm(ps, l, i, q, s, a, n, deps):
        c = 512 * l + 128 * i
        return do("t", deps + [W[l, i]], lambda e: e.matmul_mx(
            ps[:, 512 * i:512 * i + n], T.qw[:, c:c + 128], T.sw[:, c:c + 128], q[:, a:a + n], s[:, a:a + n], True, True))

    def empty(q, ps, i, a, n, u, c, deps, scale=True):
        src = ps[:, 512 * i + a:512 * i + a + n]
        out = u[:, 4 * c + i:4 * (c + n):4]
        if q == "v":
            if scale:
                return do("v", deps, lambda e: e.tensor_scalar(out, src, 0.0, C, AluOpType.max, AluOpType.mult))
            return do("v", deps, lambda e: e.tensor_scalar(out, src, 0.0, None, AluOpType.max))
        f = ActivationFunctionType.Relu
        if scale:
            return do("s", deps, lambda e: e.activation(out, src, f, scale=C))
        return do("s", deps, lambda e: e.activation(out, src, f))

    a1 = gather("v", 0, T.xu, T.g0, 192, CUT["send"], SH, [zr[0], ld["xh"]])
    a2 = gather("s", 0, T.xu, T.g0, CUT["send"], 320, SH, [zr[0], ld["xh"]])
    qa = quant(T.q0, T.s0, 256, 384, T.g0, 160, [a1, a2])
    sent = came = 0
    if not last:
        dst = T.cores[rank + 1]
        rid, pid = topo.addr(dst)[0], topo.addr(dst)[1]
        use = topo.engines(core, dst)
        half = len(use) // 2
        need("g", [qa])
        g.remote_dma(T.q0[:, 0:96].bitcast(dt.uint8), T.q0[:, 288:384].bitcast(dt.uint8), T.sem.rcv, T.sem.snt, pid, rid,
                     sum(1 << e for e in use[:half]))
        g.remote_dma(T.s0[:, 0:96], T.s0[:, 288:384], T.sem.rcv, T.sem.snt, pid, rid, sum(1 << e for e in use[half:]))
        sent = len(use)
    if not first:
        came = len(topo.engines(T.cores[rank - 1], core))
    b1 = gather("v", 0, T.xu, T.g0, 32, CUT["x"], SH, [zr[1], ld["xl"]])
    b2 = gather("s", 0, T.xu, T.g0, CUT["x"], 192, SH, [zr[1], ld["xl"], ld["xh"]])
    for n, lo in [("w1a", 2048), ("w1b", 3072), ("w2a", 4096), ("w2b", 5120)]:
        ld[n] = dma("y", "ld_" + n, [b1], T.wb[:, lo:lo + 1024], T.w[:, lo:lo + 1024])
    ld["v"] = dma("y", "ld_v", [], T.vb[:], T.v[:])
    quant_w(0, 0, 2, "w0a")
    qb = quant(T.q0, T.s0, 96, 256, T.g0, 0, [b1, b2])
    quant_w(0, 2, 4, "w0b")
    off[1] = lists(1)
    off[2] = lists(2)

    Q = [T.q0, T.q1, T.q2]
    S = [T.s0, T.s1, T.s2]
    U = [None, T.u1, T.u2, T.u3]
    own = [None, 96, 64, 0]
    halo = [64, 32, 0]

    def main_mm(l, deps):
        return [mm(T.pm, l, i, Q[l], S[l], 128, 224 - 32 * l, deps) for i in range(4)]

    def main_empty(l, tok):
        return [empty(MAIN[l][i], T.pm, i, 0, 224 - 32 * l, U[l + 1], own[l + 1] + 32 * (l + 1), [tok[i]]) for i in range(4)]

    def corner_mm(l, deps):
        a = 96 if first and l == 0 else 0
        return [mm(T.pc, l, i, Q[l], S[l], a, 128, deps) for i in range(4)]

    def corner_empty(l, tok):
        u, o = U[l + 1], own[l + 1]
        p = 0 if first and l == 0 else halo[l] + 32
        if first:
            return [], [empty(PAIR[l][i], T.pc, i, p, 32 * (l + 1), u, o, [tok[i]]) for i in range(4)]
        a, b = 256 * l, 128 * l
        r = [empty(PAIR[l][i], T.pc, i, p - 32, 64, T.fp, 64 * l, [tok[i]], scale=False) for i in range(4)]
        h, m = [], []
        if halo[l]:
            h = [empty(HALO[l][i], T.pc, i, 0, halo[l], u, 0, [tok[i], r[i]]) for i in range(4)]
        if l:
            m = [empty(REST[l][i], T.pc, i, p + 32, 32 * l, u, o + 32, [tok[i], r[i]] + h[i:i + 1]) for i in range(4)]
        add = do("v", r, lambda e: e.tensor_tensor(
            T.fs[:, b:b + 128], T.fp[:, a:a + 128], T.fp[:, a + 128:a + 256], AluOpType.add))
        m.append(do("v", [add], lambda e: e.tensor_scalar(
            u[:, 4 * o:4 * (o + 32)], T.fs[:, b:b + 128], C, None, AluOpType.mult)))
        return h, m

    tm = main_mm(0, [qa, qb])
    tc = corner_mm(0, [qb] if first else [qb, ("rcv", came)])
    em = main_empty(0, tm)
    m1 = gather("v", 1, T.u1, T.g1, 160, CUT["m1"], SH, em)
    m2 = gather("s", 1, T.u1, T.g1, CUT["m1"], 352, SH, em)
    quant_w(1, 0, 2, "w1a")
    qm = quant(T.q1, T.s1, 128, 320, T.g1, 128, [m1, m2])
    quant_w(1, 2, 4, "w1b")
    tm = main_mm(1, [qm])
    h, m = corner_empty(0, tc)
    c1 = [] if first else [gather("s", 1, T.u1, T.g1, 32, 96, SH, h + [zr[2]])]
    c1.append(gather("v", 1, T.u1, T.g1, 96, 160, SH, m + em + [zr[2]]))
    qc = quant(T.q1, T.s1, 0, 128, T.g1, 0, c1 + zr)
    tc = corner_mm(1, [qc])
    em = main_empty(1, tm)
    m1 = gather("v", 2, T.u2, T.g2, 160, CUT["m2"], SH, em)
    m2 = gather("s", 2, T.u2, T.g2, CUT["m2"], 320, SH, em)
    quant_w(2, 0, 2, "w2a")
    quant_w(2, 2, 4, "w2b")
    qm = quant(T.q2, T.s2, 128, 288, T.g2, 128, [m1, m2])
    tm = main_mm(2, [qm])
    h, m = corner_empty(1, tc)
    c1 = [] if first else [gather("s", 2, T.u2, T.g2, 32, 64, SH, h + [zr[3]])]
    c1.append(gather("s", 2, T.u2, T.g2, 64, CUT["c2"], SH, m + [zr[3]]))
    c1.append(gather("v", 2, T.u2, T.g2, CUT["c2"], 160, SH, m + em))
    qc = quant(T.q2, T.s2, 0, 128, T.g2, 0, c1 + zr)
    tc = corner_mm(2, [qc])
    em = main_empty(2, tm)
    qv = quant(T.qv, T.sv, 0, 128, T.vb, 0, [ld["v"]])
    qh = quant(T.q3, T.s3, 128, 256, T.u3, 128, em)

    def last_mm(ps, a, deps):
        return do("t", deps, lambda e: e.matmul_mx(
            ps[:, 0:128], T.qv[:], T.sv[:], T.q3[:, a:a + 128], T.s3[:, a:a + 128], True, True))
    th = last_mm(T.pm, 128, [qh, qv])
    h, m = corner_empty(2, tc)
    ql = quant(T.q3, T.s3, 0, 128, T.u3, 0, em + m)
    tl = last_mm(T.pc, 0, [ql])
    yh = do("s", [th], lambda e: e.activation(T.yt[:, 128:256], T.pm[:, 0:128], ActivationFunctionType.Copy))
    sh = dma("y", "yh", [yh], T.y[:, 128:256], T.yt[:, 128:256])
    yl = do("v", [tl], lambda e: e.tensor_copy(T.yt[:, 0:128], T.pc[:, 0:128]))
    sl = dma("y", "yl", [yl], T.y[:, 0:128], T.yt[:, 0:128])
    tail = [sh, sl] + [("q" + q, n) for q, n in done.items()]
    if not last:
        tail.append(("snt", sent))
    need("g", tail)
